import numpy as np
CORES = [0,1,2,3,4,5,6,7,128,129,130,131,132,133,134,135]
N = 16
ROOT = 8
def setup_inputs(rng):
    return {"x": rng.standard_normal((N, 128, 2), dtype=np.float32)}
def reference(x):
    return {"y": np.broadcast_to(x[ROOT], x.shape)}

@@ -1,0 +1,38 @@
+from concourse.bass import DstId, RemoteDMATransfer
+
+SCRATCH = {
+    "stage": ("dram", [128, 2], "float32"),
+    "land": ("dram", [128, 2], "float32"),
+}
+SEMAPHORES = ["loaded", "sent", "arrived", "stored"]
+
+
+def rank_program(g, core, T, topo):
+    rank = T.rank_of(core)
+    if rank is None:
+        return
+    root = T.cores[T.root]
+
+    if core != root:
+        g.wait_ge(T.sem.arrived, 1)
+        g.dma_start(T.y[:], T.land[:]).then_inc(T.sem.stored, 16)
+        g.wait_ge(T.sem.stored, 16)
+        return
+
+    g.dma_start(T.stage[:], T.x[:]).then_inc(T.sem.loaded, 16)
+
+    here = (topo.host(root), topo.chip(root))
+    others = [c for c in T.cores if c != root]
+    far = [c for c in others if (topo.host(c), topo.chip(c)) != here]
+    near = [c for c in others if (topo.host(c), topo.chip(c)) == here]
+    transfers = []
+    for engine, dst in list(enumerate(far)) + list(enumerate(near, start=8)):
+        rid, pid = topo.addr(dst, root)
+        transfers.append(RemoteDMATransfer(dst_ids=[DstId(rid=rid, pnc=pid)], dma_engine_mask=1 << engine,
+                                           remote_sem=T.sem.arrived, src=T.stage[:], dst=T.land[:]))
+
+    g.wait_ge(T.sem.loaded, 16)
+    g.remote_dma_fused(transfers, local_sem=T.sem.sent)
+    g.dma_start(T.y[:], T.x[:]).then_inc(T.sem.stored, 16)
+    g.wait_ge(T.sem.stored, 16)
+    g.wait_ge(T.sem.sent, len(transfers))

@@ -6,33 +6,49 @@ SCRATCH = {
 }
 SEMAPHORES = ["loaded", "sent", "arrived", "stored"]
 
+PLAN = (("far", 0, 4, 0x000F), ("far", 4, 8, 0x00F0), ("near", 0, 7, 0xFF00))
+
+
+def engines(mask):
+    return bin(mask).count("1")
+
 
 def rank_program(g, core, T, topo):
     rank = T.rank_of(core)
     if rank is None:
         return
     root = T.cores[T.root]
+    here = (topo.host(root), topo.chip(root))
+    others = [c for c in T.cores if c != root]
+    groups = {
+        "far": [c for c in others if (topo.host(c), topo.chip(c)) != here],
+        "near": [c for c in others if (topo.host(c), topo.chip(c)) == here],
+    }
 
     if core != root:
-        g.wait_ge(T.sem.arrived, 1)
+        for name, lo, hi, mask in PLAN:
+            if core in groups[name][lo:hi]:
+                g.wait_ge(T.sem.arrived, engines(mask))
         g.dma_start(T.y[:], T.land[:]).then_inc(T.sem.stored, 16)
         g.wait_ge(T.sem.stored, 16)
         return
 
     g.dma_start(T.stage[:], T.x[:]).then_inc(T.sem.loaded, 16)
-
-    here = (topo.host(root), topo.chip(root))
-    others = [c for c in T.cores if c != root]
-    far = [c for c in others if (topo.host(c), topo.chip(c)) != here]
-    near = [c for c in others if (topo.host(c), topo.chip(c)) == here]
     transfers = []
-    for engine, dst in list(enumerate(far)) + list(enumerate(near, start=8)):
-        rid, pid = topo.addr(dst, root)
-        transfers.append(RemoteDMATransfer(dst_ids=[DstId(rid=rid, pnc=pid)], dma_engine_mask=1 << engine,
-                                           remote_sem=T.sem.arrived, src=T.stage[:], dst=T.land[:]))
+    total = 0
+    for name, lo, hi, mask in PLAN:
+        ids = []
+        outs = []
+        for dst in groups[name][lo:hi]:
+            rid, pid = topo.addr(dst, root)
+            ids.append(DstId(rid=rid, pnc=pid))
+            outs.append(T.land[:])
+        transfers.append(RemoteDMATransfer(dst_ids=ids, dma_engine_mask=mask, remote_sem=T.sem.arrived,
+                                           srcs=[T.stage[:]], dsts=outs))
+        total += engines(mask)
 
     g.wait_ge(T.sem.loaded, 16)
     g.remote_dma_fused(transfers, local_sem=T.sem.sent)
     g.dma_start(T.y[:], T.x[:]).then_inc(T.sem.stored, 16)
     g.wait_ge(T.sem.stored, 16)
-    g.wait_ge(T.sem.sent, len(transfers))
+    g.wait_ge(T.sem.sent, total)

@@ -6,7 +6,7 @@ SCRATCH = {
 }
 SEMAPHORES = ["loaded", "sent", "arrived", "stored"]
 
-PLAN = (("far", 0, 4, 0x000F), ("far", 4, 8, 0x00F0), ("near", 0, 7, 0xFF00))
+PLAN = ((0, 15, 0x00FF),)
 
 
 def engines(mask):
@@ -20,14 +20,12 @@ def rank_program(g, core, T, topo):
     root = T.cores[T.root]
     here = (topo.host(root), topo.chip(root))
     others = [c for c in T.cores if c != root]
-    groups = {
-        "far": [c for c in others if (topo.host(c), topo.chip(c)) != here],
-        "near": [c for c in others if (topo.host(c), topo.chip(c)) == here],
-    }
+    order = ([c for c in others if (topo.host(c), topo.chip(c)) != here]
+             + [c for c in others if (topo.host(c), topo.chip(c)) == here])
 
     if core != root:
-        for name, lo, hi, mask in PLAN:
-            if core in groups[name][lo:hi]:
+        for lo, hi, mask in PLAN:
+            if core in order[lo:hi]:
                 g.wait_ge(T.sem.arrived, engines(mask))
         g.dma_start(T.y[:], T.land[:]).then_inc(T.sem.stored, 16)
         g.wait_ge(T.sem.stored, 16)
@@ -36,10 +34,10 @@ def rank_program(g, core, T, topo):
     g.dma_start(T.stage[:], T.x[:]).then_inc(T.sem.loaded, 16)
     transfers = []
     total = 0
-    for name, lo, hi, mask in PLAN:
+    for lo, hi, mask in PLAN:
         ids = []
         outs = []
-        for dst in groups[name][lo:hi]:
+        for dst in order[lo:hi]:
             rid, pid = topo.addr(dst, root)
             ids.append(DstId(rid=rid, pnc=pid))
             outs.append(T.land[:])

@@ -6,11 +6,8 @@ SCRATCH = {
 }
 SEMAPHORES = ["loaded", "sent", "arrived", "stored"]
 
-PLAN = ((0, 15, 0x00FF),)
-
-
-def engines(mask):
-    return bin(mask).count("1")
+MASK = 0x00FF
+ENGINES = 8
 
 
 def rank_program(g, core, T, topo):
@@ -18,35 +15,29 @@ def rank_program(g, core, T, topo):
     if rank is None:
         return
     root = T.cores[T.root]
-    here = (topo.host(root), topo.chip(root))
-    others = [c for c in T.cores if c != root]
-    order = ([c for c in others if (topo.host(c), topo.chip(c)) != here]
-             + [c for c in others if (topo.host(c), topo.chip(c)) == here])
 
     if core != root:
-        for lo, hi, mask in PLAN:
-            if core in order[lo:hi]:
-                g.wait_ge(T.sem.arrived, engines(mask))
+        g.wait_ge(T.sem.arrived, ENGINES)
         g.dma_start(T.y[:], T.land[:]).then_inc(T.sem.stored, 16)
         g.wait_ge(T.sem.stored, 16)
         return
 
     g.dma_start(T.stage[:], T.x[:]).then_inc(T.sem.loaded, 16)
-    transfers = []
-    total = 0
-    for lo, hi, mask in PLAN:
-        ids = []
-        outs = []
-        for dst in order[lo:hi]:
-            rid, pid = topo.addr(dst, root)
-            ids.append(DstId(rid=rid, pnc=pid))
-            outs.append(T.land[:])
-        transfers.append(RemoteDMATransfer(dst_ids=ids, dma_engine_mask=mask, remote_sem=T.sem.arrived,
-                                           srcs=[T.stage[:]], dsts=outs))
-        total += engines(mask)
+
+    def shortness(c):
+        on_chip = (topo.host(c), topo.chip(c)) == (topo.host(root), topo.chip(root))
+        return (on_chip, topo.die(c) == topo.die(root), c)
+
+    ids = []
+    outs = []
+    for dst in sorted([c for c in T.cores if c != root], key=shortness):
+        rid, pid = topo.addr(dst, root)
+        ids.append(DstId(rid=rid, pnc=pid))
+        outs.append(T.land[:])
+    copies = RemoteDMATransfer(dst_ids=ids, dma_engine_mask=MASK, remote_sem=T.sem.arrived, srcs=[T.stage[:]], dsts=outs)
 
     g.wait_ge(T.sem.loaded, 16)
-    g.remote_dma_fused(transfers, local_sem=T.sem.sent)
+    g.remote_dma_fused([copies], local_sem=T.sem.sent)
+    g.wait_ge(T.sem.sent, ENGINES)
     g.dma_start(T.y[:], T.x[:]).then_inc(T.sem.stored, 16)
     g.wait_ge(T.sem.stored, 16)
-    g.wait_ge(T.sem.sent, total)

from concourse.bass import DstId, RemoteDMATransfer

SCRATCH = {
    "stage": ("dram", [128, 2], "float32"),
    "land": ("dram", [128, 2], "float32"),
}
SEMAPHORES = ["loaded", "sent", "arrived", "stored"]

MASK = 0x00FF
ENGINES = 8


def rank_program(g, core, T, topo):
    rank = T.rank_of(core)
    if rank is None:
        return
    root = T.cores[T.root]

    if core != root:
        g.wait_ge(T.sem.arrived, ENGINES)
        g.dma_start(T.y[:], T.land[:]).then_inc(T.sem.stored, 16)
        g.wait_ge(T.sem.stored, 16)
        return

    g.dma_start(T.stage[:], T.x[:]).then_inc(T.sem.loaded, 16)

    def shortness(c):
        on_chip = (topo.host(c), topo.chip(c)) == (topo.host(root), topo.chip(root))
        return (on_chip, topo.die(c) == topo.die(root), c)

    ids = []
    outs = []
    for dst in sorted([c for c in T.cores if c != root], key=shortness):
        rid, pid = topo.addr(dst, root)
        ids.append(DstId(rid=rid, pnc=pid))
        outs.append(T.land[:])
    copies = RemoteDMATransfer(dst_ids=ids, dma_engine_mask=MASK, remote_sem=T.sem.arrived, srcs=[T.stage[:]], dsts=outs)

    g.wait_ge(T.sem.loaded, 16)
    g.remote_dma_fused([copies], local_sem=T.sem.sent)
    g.wait_ge(T.sem.sent, ENGINES)
    g.dma_start(T.y[:], T.x[:]).then_inc(T.sem.stored, 16)
    g.wait_ge(T.sem.stored, 16)
